import numpy as np
import ml_dtypes


def mxq(x, axis, fmt="e4m3"):
    dtype, down = {"e4m3": (ml_dtypes.float8_e4m3fn, 7), "e5m2": (ml_dtypes.float8_e5m2, 14)}[fmt]
    v = np.moveaxis(np.asarray(x, np.float32).astype(ml_dtypes.bfloat16).astype(np.float64), axis, -1)
    blocks = v.reshape(v.shape[:-1] + (-1, 32))
    amax = np.abs(blocks).max(-1, keepdims=True)
    byte = np.maximum(np.where(amax > 0, np.frexp(amax)[1] - 1 + 127, 0) - down, 1)
    scale = np.exp2(byte - 127.0)
    codes = (blocks / scale).astype(np.float32).astype(dtype).astype(np.float64)
    return np.moveaxis((codes * scale).reshape(v.shape), -1, axis)


WIDE = False


def mx_kscale(k):
    if not WIDE:
        return np.ones(k)
    levels = np.array([30, -30])
    if k % 512:
        return np.exp2(np.random.permutation(np.resize(levels, k // 32))).repeat(32)
    a = np.empty((k // 512, 16))
    for p in range(k // 512):
        a[p, :8] = np.random.permutation(np.resize(levels, 8))
        for g in range(8):
            far = levels[np.abs(levels - a[p, g]) >= 10]
            a[p, g + 8] = far[np.random.randint(len(far))]
    return np.exp2(a.ravel()).repeat(32)


def f64(x):
    return np.asarray(x).astype(np.float64)


def striped(idx):
    return np.tile(np.asarray(idx).reshape(-1, 16).T, (8, 1)).astype(np.uint16)


def unstriped(offs):
    return offs[:16].T.reshape(-1).astype(np.int64)


E2M1 = np.array([0.0, 0.5, 1.0, 1.5, 2.0, 3.0, 4.0, 6.0, -0.0, -0.5, -1.0, -1.5, -2.0, -3.0, -4.0, -6.0])


def pack_weight(w, fmt):
    k, n = w.shape
    w = f64(np.asarray(w, np.float32).astype(ml_dtypes.bfloat16)).reshape(k // 32, 32, n)
    amax = np.abs(w).max(1)
    if fmt in ("e4m3", "e5m2"):
        byte = np.frexp(amax)[1] - 1 + 127 - (7 if fmt == "e4m3" else 14)
    else:
        mant, ex = np.frexp(amax / 6.0)
        byte = np.where(mant > 0.5, ex, ex - 1) + 127
    byte = np.clip(np.where(amax > 0, byte, 1), 1, 254)
    scaled = (w * np.exp2(127.0 - byte)[:, None, :]).reshape(k, n).astype(np.float32)
    by_word = np.ascontiguousarray(scaled.reshape(k // 512, 128, 4, n).transpose(0, 1, 3, 2))
    if fmt in ("e4m3", "e5m2"):
        words = by_word.astype(ml_dtypes.float8_e4m3fn if fmt == "e4m3" else ml_dtypes.float8_e5m2).view(np.uint8)
    else:
        c = by_word.astype(ml_dtypes.float4_e2m1fn).view(np.uint8) & 0xF
        words = (c[..., 0::2] | (c[..., 1::2] << 4)).reshape(k // 512, 128, 2 * n)
    return np.ascontiguousarray(words), np.ascontiguousarray(byte.astype(np.uint8).reshape(k // 512, 16, n))


def unpack_weight(words, scales, fmt):
    g, _, n = scales.shape
    words = np.ascontiguousarray(words).reshape(g, 128, n, -1)
    if fmt in ("e4m3", "e5m2"):
        vals = words.view(ml_dtypes.float8_e4m3fn if fmt == "e4m3" else ml_dtypes.float8_e5m2).astype(np.float64)
    else:
        nib = np.empty((g, 128, n, 4), np.uint8)
        nib[..., 0::2] = words & 0xF
        nib[..., 1::2] = words >> 4
        vals = E2M1[nib]
    vals = vals * np.repeat(np.exp2(scales.astype(np.float64) - 127.0), 8, axis=1)[..., None]
    return vals.transpose(0, 1, 3, 2).reshape(g * 512, n)


K, T, J, I, R, C, G, Q = 512, 512, 256, 256, 512, 512, 32, 512


def setup_inputs():
    n = np.random.standard_normal
    idx = np.random.permutation(T)[:J]
    idx2 = np.random.permutation(C)[:J]
    idx3 = np.random.permutation(T)[:I]
    idx4 = np.random.permutation(Q)[:I]
    fk = mx_kscale(K)
    fr = mx_kscale(R)
    xtp = pack_weight(n((K, T)) / fk[:, None], "e2m1")
    wap = pack_weight(n((K, R)) * 0.5 / np.sqrt(K) * fk[:, None] * fr, "e2m1")
    wbp = pack_weight(n((K, R)) * 1 / np.sqrt(K) * fk[:, None] / fr, "e5m2")
    return {
        "xt_words": xtp[0],
        "xt_scales": xtp[1],
        "wa_words": wap[0],
        "wa_scales": wap[1],
        "tf": (n((R, C))).astype(np.float32),
        "wb_words": wbp[0],
        "wb_scales": wbp[1],
        "tv": (1.0 * n((J, Q))).astype(np.float32),
        "offs": striped(idx),
        "offs2": striped(idx2),
        "offs3": striped(idx3),
        "offs4": striped(idx4),
    }


def reference(xt_words, xt_scales, wa_words, wa_scales, tf, wb_words, wb_scales, tv, offs, offs2, offs3, offs4):
    idx = unstriped(offs)
    idx2 = unstriped(offs2)
    idx3 = unstriped(offs3)
    idx4 = unstriped(offs4)
    xtu = unpack_weight(xt_words, xt_scales, "e2m1")
    wau = unpack_weight(wa_words, wa_scales, "e2m1")
    wbu = unpack_weight(wb_words, wb_scales, "e5m2")
    xtidxg = xtu[:, idx]
    za = wau.T @ xtidxg
    ha = za * f64(tf)[:, idx2]
    xtidx3g = xtu[:, idx3]
    zb = wbu.T @ xtidx3g
    mb1 = zb.reshape(R, G, I // G).mean(axis=2)
    mb2 = np.repeat(mb1, I // G, axis=1)
    hb = zb - mb2
    haq = mxq(ha, 0, "e5m2")
    hbq = mxq(hb, 0, "e4m3")
    a0 = haq.T @ hbq
    y = np.tanh(0.04 * a0) * f64(tv)[:, idx4]
    return y

@@ -1,0 +1,179 @@
+from contextlib import ExitStack
+
+import concourse.mybir as mybir
+
+F32 = mybir.dt.float32
+BF16 = mybir.dt.bfloat16
+I32 = mybir.dt.int32
+U32 = mybir.dt.uint32
+U16 = mybir.dt.uint16
+U8 = mybir.dt.uint8
+E2M1 = mybir.dt.float4_e2m1fn_x4
+E5M2 = mybir.dt.float8_e5m2_x4
+E4M3 = mybir.dt.float8_e4m3fn_x4
+ALU = mybir.AluOpType
+ACT = mybir.ActivationFunctionType
+
+P = 128
+K, T, J, I, R, C, Q = 512, 512, 256, 256, 512, 512, 512
+SLOTS = 4
+RUN = 8
+BUNDLE = 8
+HALF = 128
+HALVES = 2
+
+FLOPS = 2 * K * R * J + 2 * K * R * I + 2 * R * J * I
+
+
+def tile_list_meet_timestable_levelled_tabled_kernel(
+    tc, xt_words, xt_scales, wa_words, wa_scales, tf, wb_words, wb_scales, tv, offs, offs2, offs3, offs4, out
+):
+    nc = tc.nc
+    with ExitStack() as ctx:
+        sb = ctx.enter_context(tc.tile_pool(name="sb", bufs=1))
+        ps = ctx.enter_context(tc.psum_pool(name="ps", bufs=1))
+
+        def load_list(name, src):
+            tile = sb.tile([P, 16], U16, name=name)
+            nc.sync.dma_start(tile[:], src)
+            return tile
+
+        def load_scales(name, src):
+            plane = sb.tile([P, R], U8, name=name, align_bytes=64)
+            for q in range(4):
+                nc.sync.dma_start(
+                    plane[32 * q : 32 * q + 32, :].bitcast(I32),
+                    src[:, 4 * q : 4 * q + 4, :].bitcast(I32).to_broadcast([8, 4, R // 4]),
+                )
+            return plane
+
+        list_b = load_list("list_b", offs3)
+        xt_w = sb.tile([P, T], U16, name="xt_w", align_bytes=64)
+        nc.sync.dma_start(xt_w[:].bitcast(I32), xt_words[0].bitcast(I32))
+        list_a = load_list("list_a", offs)
+        xt_s = load_scales("xt_s", xt_scales)
+        wb_w_raw = sb.tile([P, R], U32, name="wb_w_raw", align_bytes=64)
+        nc.sync.dma_start(wb_w_raw[:].bitcast(I32), wb_words[0].rearrange("p c t -> p (c t)").bitcast(I32))
+        wb_s_raw = load_scales("wb_s_raw", wb_scales)
+        list_f = load_list("list_f", offs2)
+        tf_rows = tf.rearrange("(b t m) c -> t b m c", t=SLOTS, m=RUN)
+
+        def load_factors(t):
+            tile = sb.tile([P, C], F32, name="tf%d" % t)
+            nc.sync.dma_start(tile[:], tf_rows[t])
+            return tile
+
+        tf_sb = [load_factors(0), load_factors(1)]
+        wa_w_raw = sb.tile([P, R], U16, name="wa_w_raw", align_bytes=64)
+        nc.sync.dma_start(wa_w_raw[:].bitcast(I32), wa_words[0].bitcast(I32))
+        wa_s_raw = load_scales("wa_s_raw", wa_scales)
+        tf_sb.extend([load_factors(2), load_factors(3)])
+        list_v = load_list("list_v", offs4)
+        tv_sb = sb.tile([P, HALVES, Q], F32, name="tv_sb")
+        nc.sync.dma_start(tv_sb[:], tv.rearrange("(h p) q -> p h q", p=P))
+
+        def deal(name, raw, dtype):
+            dealt = sb.tile([P, R], dtype, name=name, align_bytes=64)
+            nc.scalar.copy(
+                dealt[:].bitcast(U32).rearrange("p (t b w) -> p t b w", t=SLOTS, b=R // 32),
+                raw[:].bitcast(U32).rearrange("p (b t w) -> p t b w", t=SLOTS, b=R // 32),
+            )
+            return dealt
+
+        def pick(name, window, dtype, entries):
+            picked = sb.tile([P, J], dtype, name=name, align_bytes=64)
+            nc.vector.tensor_copy(picked[:], window[:].indirect(entries[:]))
+            return picked
+
+        def first_products(name, w_words, w_fmt, w_scales, x_words, x_scales):
+            banks = []
+            for h in range(HALVES):
+                bank = ps.tile([P, SLOTS, HALF], F32, name="%s%d" % (name, h))
+                cols = slice(h * HALF, (h + 1) * HALF)
+                for t in range(SLOTS):
+                    rows = slice(t * P, (t + 1) * P)
+                    nc.tensor.matmul_mx(
+                        out=bank[:, t, :],
+                        lhsT=w_words[:, rows].bitcast(w_fmt),
+                        lhsT_scale=w_scales[:, rows],
+                        rhs=x_words[:, cols].bitcast(E2M1),
+                        rhs_scale=x_scales[:, cols],
+                        start=True,
+                        stop=True,
+                    )
+                banks.append(bank)
+            return banks
+
+        xb_w = pick("xb_w", xt_w, U16, list_b)
+        xa_w = pick("xa_w", xt_w, U16, list_a)
+        xb_s = pick("xb_s", xt_s, U8, list_b)
+        xa_s = pick("xa_s", xt_s, U8, list_a)
+        wb_w = deal("wb_w", wb_w_raw, U32)
+        wb_s = deal("wb_s", wb_s_raw, U8)
+        zb = first_products("zb", wb_w, E5M2, wb_s, xb_w, xb_s)
+
+        wa_w = deal("wa_w", wa_w_raw, U16)
+        wa_s = deal("wa_s", wa_s_raw, U8)
+        za = first_products("za", wa_w, E2M1, wa_s, xa_w, xa_s)
+
+        tf_picked = sb.tile([P, SLOTS, J], F32, name="tf_picked")
+        for t in range(SLOTS):
+            nc.scalar.activation(tf_picked[:, t, :], tf_sb[t][:].indirect(list_f[:]), ACT.Copy)
+        tv_picked = sb.tile([P, HALVES, I], F32, name="tv_picked")
+        for h in range(HALVES):
+            nc.scalar.activation(tv_picked[:, h, :], tv_sb[:, h, :].indirect(list_v[:]), ACT.Copy)
+
+        groups = HALF // BUNDLE
+        sums, means, hb = [], [], []
+        for h in range(HALVES):
+            total = sb.tile([P, SLOTS, groups], F32, name="sums%d" % h)
+            nc.vector.tensor_reduce(
+                total[:], zb[h][:].rearrange("p t (g m) -> p t g m", m=BUNDLE), mybir.AxisListType.X, ALU.add
+            )
+            sums.append(total)
+        for h in range(HALVES):
+            mean = sb.tile([P, SLOTS, groups], F32, name="means%d" % h)
+            nc.vector.tensor_scalar(mean[:], sums[h][:], 1.0 / BUNDLE, None, ALU.mult)
+            means.append(mean)
+        for h in range(HALVES):
+            centred = sb.tile([P, HALF * SLOTS], BF16, name="hb%d" % h, align_bytes=64)
+            nc.vector.tensor_tensor(
+                centred[:].rearrange("p (g m t) -> p g m t", m=BUNDLE, t=SLOTS),
+                zb[h][:].rearrange("p t (g m) -> p g m t", m=BUNDLE),
+                means[h][:].rearrange("p t g -> p g t").unsqueeze(2).to_broadcast([P, groups, BUNDLE, SLOTS]),
+                ALU.subtract,
+            )
+            hb.append(centred)
+        hb_w = sb.tile([P, I], U32, name="hb_w", align_bytes=64)
+        hb_s = sb.tile([P, I], U8, name="hb_s", align_bytes=64)
+        ha = []
+        for h in range(HALVES):
+            cols = slice(h * HALF, (h + 1) * HALF)
+            nc.vector.quantize_mx(out=hb_w[:, cols].bitcast(E4M3), scales=hb_s[:, cols], in_=hb[h][:])
+            scaled = sb.tile([P, HALF * SLOTS], BF16, name="ha%d" % h, align_bytes=64)
+            nc.vector.tensor_tensor(
+                scaled[:].rearrange("p (j t) -> p j t", t=SLOTS),
+                za[h][:].rearrange("p t j -> p j t"),
+                tf_picked[:, :, cols].rearrange("p t j -> p j t"),
+                ALU.mult,
+            )
+            ha.append(scaled)
+        for h in range(HALVES):
+            ha_w = sb.tile([P, HALF], U32, name="ha_w%d" % h, align_bytes=64)
+            ha_s = sb.tile([P, HALF], U8, name="ha_s%d" % h, align_bytes=64)
+            nc.vector.quantize_mx(out=ha_w[:].bitcast(E5M2), scales=ha_s[:], in_=ha[h][:])
+            score = ps.tile([P, I], F32, name="score%d" % h)
+            nc.tensor.matmul_mx(
+                out=score[:],
+                lhsT=ha_w[:].bitcast(E5M2),
+                lhsT_scale=ha_s[:],
+                rhs=hb_w[:].bitcast(E4M3),
+                rhs_scale=hb_s[:],
+                start=True,
+                stop=True,
+            )
+            squashed = sb.tile([P, I], F32, name="squashed%d" % h)
+            nc.scalar.activation(squashed[:], score[:], ACT.Tanh, scale=0.04)
+            result = sb.tile([P, I], F32, name="result%d" % h)
+            nc.vector.tensor_tensor(result[:], squashed[:], tv_picked[:, h, :], ALU.mult)
+            nc.sync.dma_start(out[h * HALF : (h + 1) * HALF, :], result[:])

@@ -47,30 +47,33 @@ def tile_list_meet_timestable_levelled_tabled_kernel(
                 )
             return plane
 
-        list_b = load_list("list_b", offs3)
-        xt_w = sb.tile([P, T], U16, name="xt_w", align_bytes=64)
-        nc.sync.dma_start(xt_w[:].bitcast(I32), xt_words[0].bitcast(I32))
-        list_a = load_list("list_a", offs)
-        xt_s = load_scales("xt_s", xt_scales)
-        wb_w_raw = sb.tile([P, R], U32, name="wb_w_raw", align_bytes=64)
-        nc.sync.dma_start(wb_w_raw[:].bitcast(I32), wb_words[0].rearrange("p c t -> p (c t)").bitcast(I32))
-        wb_s_raw = load_scales("wb_s_raw", wb_scales)
-        list_f = load_list("list_f", offs2)
         tf_rows = tf.rearrange("(b t m) c -> t b m c", t=SLOTS, m=RUN)
+        tf_sb = []
 
         def load_factors(t):
             tile = sb.tile([P, C], F32, name="tf%d" % t)
             nc.sync.dma_start(tile[:], tf_rows[t])
             return tile
 
-        tf_sb = [load_factors(0), load_factors(1)]
+        list_b = load_list("list_b", offs3)
+        xt_w = sb.tile([P, T], U16, name="xt_w", align_bytes=64)
+        nc.sync.dma_start(xt_w[:].bitcast(I32), xt_words[0].bitcast(I32))
+        xt_s = load_scales("xt_s", xt_scales)
+        wb_w_raw = sb.tile([P, R], U32, name="wb_w_raw", align_bytes=64)
+        nc.sync.dma_start(wb_w_raw[:].bitcast(I32), wb_words[0].rearrange("p c t -> p (c t)").bitcast(I32))
+        tf_sb.append(load_factors(0))
+        wb_s_raw = load_scales("wb_s_raw", wb_scales)
+        list_a = load_list("list_a", offs)
+        list_f = load_list("list_f", offs2)
+        tf_sb.append(load_factors(1))
+        tf_sb.append(load_factors(2))
         wa_w_raw = sb.tile([P, R], U16, name="wa_w_raw", align_bytes=64)
         nc.sync.dma_start(wa_w_raw[:].bitcast(I32), wa_words[0].bitcast(I32))
         wa_s_raw = load_scales("wa_s_raw", wa_scales)
-        tf_sb.extend([load_factors(2), load_factors(3)])
-        list_v = load_list("list_v", offs4)
-        tv_sb = sb.tile([P, HALVES, Q], F32, name="tv_sb")
+        tf_sb.append(load_factors(3))
+        tv_sb = sb.tile([P, HALVES, Q], F32, name="tv_sb", tag="tv")
         nc.sync.dma_start(tv_sb[:], tv.rearrange("(h p) q -> p h q", p=P))
+        list_v = load_list("list_v", offs4)
 
         def deal(name, raw, dtype):
             dealt = sb.tile([P, R], dtype, name=name, align_bytes=64)
@@ -105,8 +108,8 @@ def tile_list_meet_timestable_levelled_tabled_kernel(
             return banks
 
         xb_w = pick("xb_w", xt_w, U16, list_b)
-        xa_w = pick("xa_w", xt_w, U16, list_a)
         xb_s = pick("xb_s", xt_s, U8, list_b)
+        xa_w = pick("xa_w", xt_w, U16, list_a)
         xa_s = pick("xa_s", xt_s, U8, list_a)
         wb_w = deal("wb_w", wb_w_raw, U32)
         wb_s = deal("wb_s", wb_s_raw, U8)
@@ -126,54 +129,59 @@ def tile_list_meet_timestable_levelled_tabled_kernel(
         groups = HALF // BUNDLE
         sums, means, hb = [], [], []
         for h in range(HALVES):
-            total = sb.tile([P, SLOTS, groups], F32, name="sums%d" % h)
+            total = sb.tile([P, groups, SLOTS], F32, name="sums%d" % h)
             nc.vector.tensor_reduce(
-                total[:], zb[h][:].rearrange("p t (g m) -> p t g m", m=BUNDLE), mybir.AxisListType.X, ALU.add
+                total[:], zb[h][:].rearrange("p t (g m) -> p g t m", m=BUNDLE), mybir.AxisListType.X, ALU.add
             )
             sums.append(total)
         for h in range(HALVES):
-            mean = sb.tile([P, SLOTS, groups], F32, name="means%d" % h)
-            nc.vector.tensor_scalar(mean[:], sums[h][:], 1.0 / BUNDLE, None, ALU.mult)
+            mean = sb.tile([P, groups, SLOTS], F32, name="means%d" % h)
+            nc.gpsimd.tensor_scalar(mean[:], sums[h][:], 1.0 / BUNDLE, 0.0, ALU.mult, ALU.add)
             means.append(mean)
         for h in range(HALVES):
             centred = sb.tile([P, HALF * SLOTS], BF16, name="hb%d" % h, align_bytes=64)
             nc.vector.tensor_tensor(
                 centred[:].rearrange("p (g m t) -> p g m t", m=BUNDLE, t=SLOTS),
                 zb[h][:].rearrange("p t (g m) -> p g m t", m=BUNDLE),
-                means[h][:].rearrange("p t g -> p g t").unsqueeze(2).to_broadcast([P, groups, BUNDLE, SLOTS]),
+                means[h][:].unsqueeze(2).to_broadcast([P, groups, BUNDLE, SLOTS]),
                 ALU.subtract,
             )
             hb.append(centred)
         hb_w = sb.tile([P, I], U32, name="hb_w", align_bytes=64)
         hb_s = sb.tile([P, I], U8, name="hb_s", align_bytes=64)
-        ha = []
         for h in range(HALVES):
             cols = slice(h * HALF, (h + 1) * HALF)
             nc.vector.quantize_mx(out=hb_w[:, cols].bitcast(E4M3), scales=hb_s[:, cols], in_=hb[h][:])
-            scaled = sb.tile([P, HALF * SLOTS], BF16, name="ha%d" % h, align_bytes=64)
-            nc.vector.tensor_tensor(
-                scaled[:].rearrange("p (j t) -> p j t", t=SLOTS),
-                za[h][:].rearrange("p t j -> p j t"),
-                tf_picked[:, :, cols].rearrange("p t j -> p j t"),
-                ALU.mult,
-            )
-            ha.append(scaled)
         for h in range(HALVES):
+            rows = slice(h * HALF, (h + 1) * HALF)
+            ha = sb.tile([P, HALF * SLOTS], BF16, name="ha%d" % h, align_bytes=64)
+            width = HALF if h < HALVES - 1 else HALF // 2
+            for start in range(0, HALF, width):
+                nc.vector.tensor_tensor(
+                    ha[:, start * SLOTS : (start + width) * SLOTS].rearrange("p (c e t) -> p c t e", e=4, t=SLOTS),
+                    za[h][:, :, start : start + width].rearrange("p t (c e) -> p c t e", e=4),
+                    tf_picked[:, :, h * HALF + start : h * HALF + start + width].rearrange("p t (c e) -> p c t e", e=4),
+                    ALU.mult,
+                )
             ha_w = sb.tile([P, HALF], U32, name="ha_w%d" % h, align_bytes=64)
             ha_s = sb.tile([P, HALF], U8, name="ha_s%d" % h, align_bytes=64)
-            nc.vector.quantize_mx(out=ha_w[:].bitcast(E5M2), scales=ha_s[:], in_=ha[h][:])
-            score = ps.tile([P, I], F32, name="score%d" % h)
-            nc.tensor.matmul_mx(
-                out=score[:],
-                lhsT=ha_w[:].bitcast(E5M2),
-                lhsT_scale=ha_s[:],
-                rhs=hb_w[:].bitcast(E4M3),
-                rhs_scale=hb_s[:],
-                start=True,
-                stop=True,
-            )
-            squashed = sb.tile([P, I], F32, name="squashed%d" % h)
-            nc.scalar.activation(squashed[:], score[:], ACT.Tanh, scale=0.04)
+            nc.vector.quantize_mx(out=ha_w[:].bitcast(E5M2), scales=ha_s[:], in_=ha[:])
             result = sb.tile([P, I], F32, name="result%d" % h)
-            nc.vector.tensor_tensor(result[:], squashed[:], tv_picked[:, h, :], ALU.mult)
+            width = I if h < HALVES - 1 else HALF
+            for start in range(0, I, width):
+                cols = slice(start, start + width)
+                score = ps.tile([P, width], F32, name="score%d_%d" % (h, start))
+                nc.tensor.matmul_mx(
+                    out=score[:],
+                    lhsT=ha_w[:].bitcast(E5M2),
+                    lhsT_scale=ha_s[:],
+                    rhs=hb_w[:, cols].bitcast(E4M3),
+                    rhs_scale=hb_s[:, cols],
+                    start=True,
+                    stop=True,
+                )
+                name = "squashed%d_%d" % (h, start)
+                squashed = sb.tile([P, width], F32, name=name, tag="tv" if h == 0 else name)
+                nc.scalar.activation(squashed[:], score[:], ACT.Tanh, scale=0.04)
+                nc.vector.tensor_tensor(result[:, cols], squashed[:], tv_picked[:, h, cols], ALU.mult)
             nc.sync.dma_start(out[h * HALF : (h + 1) * HALF, :], result[:])

@@ -55,33 +55,38 @@ def tile_list_meet_timestable_levelled_tabled_kernel(
             nc.sync.dma_start(tile[:], tf_rows[t])
             return tile
 
+        wb_rows = wb_scales.bitcast(I32)
+        wb_s_low = sb.tile([P, R], U8, name="wb_s_low", align_bytes=64)
+        wb_s_high = sb.tile([P, R], U8, name="wb_s_high", align_bytes=64)
+        nc.gpsimd.dma_start(wb_s_high[58:128, :].bitcast(I32), wb_rows[:, 2:16, :].to_broadcast([5, 14, R // 4]))
         list_b = load_list("list_b", offs3)
         xt_w = sb.tile([P, T], U16, name="xt_w", align_bytes=64)
         nc.sync.dma_start(xt_w[:].bitcast(I32), xt_words[0].bitcast(I32))
         xt_s = load_scales("xt_s", xt_scales)
         wb_w_raw = sb.tile([P, R], U32, name="wb_w_raw", align_bytes=64)
         nc.sync.dma_start(wb_w_raw[:].bitcast(I32), wb_words[0].rearrange("p c t -> p (c t)").bitcast(I32))
-        tf_sb.append(load_factors(0))
-        wb_s_raw = load_scales("wb_s_raw", wb_scales)
+        nc.sync.dma_start(wb_s_low[0:70, :].bitcast(I32), wb_rows[:, 0:14, :].to_broadcast([5, 14, R // 4]))
         list_a = load_list("list_a", offs)
         list_f = load_list("list_f", offs2)
+        tf_sb.append(load_factors(0))
         tf_sb.append(load_factors(1))
-        tf_sb.append(load_factors(2))
         wa_w_raw = sb.tile([P, R], U16, name="wa_w_raw", align_bytes=64)
         nc.sync.dma_start(wa_w_raw[:].bitcast(I32), wa_words[0].bitcast(I32))
         wa_s_raw = load_scales("wa_s_raw", wa_scales)
+        tf_sb.append(load_factors(2))
         tf_sb.append(load_factors(3))
-        tv_sb = sb.tile([P, HALVES, Q], F32, name="tv_sb", tag="tv")
-        nc.sync.dma_start(tv_sb[:], tv.rearrange("(h p) q -> p h q", p=P))
         list_v = load_list("list_v", offs4)
+        tv_sb = []
+        for h in range(HALVES):
+            tile = sb.tile([P, Q], F32, name="tv%d" % h, tag="tv%d" % h)
+            nc.sync.dma_start(tile[:], tv[h * HALF : (h + 1) * HALF, :])
+            tv_sb.append(tile)
 
-        def deal(name, raw, dtype):
-            dealt = sb.tile([P, R], dtype, name=name, align_bytes=64)
+        def deal(dealt, raw):
             nc.scalar.copy(
-                dealt[:].bitcast(U32).rearrange("p (t b w) -> p t b w", t=SLOTS, b=R // 32),
-                raw[:].bitcast(U32).rearrange("p (b t w) -> p t b w", t=SLOTS, b=R // 32),
+                dealt.bitcast(U32).rearrange("p (t b w) -> p t b w", t=SLOTS, b=R // 32),
+                raw.bitcast(U32).rearrange("p (b t w) -> p t b w", t=SLOTS, b=R // 32),
             )
-            return dealt
 
         def pick(name, window, dtype, entries):
             picked = sb.tile([P, J], dtype, name=name, align_bytes=64)
@@ -111,20 +116,24 @@ def tile_list_meet_timestable_levelled_tabled_kernel(
         xb_s = pick("xb_s", xt_s, U8, list_b)
         xa_w = pick("xa_w", xt_w, U16, list_a)
         xa_s = pick("xa_s", xt_s, U8, list_a)
-        wb_w = deal("wb_w", wb_w_raw, U32)
-        wb_s = deal("wb_s", wb_s_raw, U8)
+        wb_w = sb.tile([P, R], U32, name="wb_w", align_bytes=64)
+        wb_s = sb.tile([P, R], U8, name="wb_s", align_bytes=64)
+        deal(wb_w[:], wb_w_raw[:])
+        deal(wb_s[0:64, :], wb_s_low[0:64, :])
+        deal(wb_s[64:128, :], wb_s_high[64:128, :])
         zb = first_products("zb", wb_w, E5M2, wb_s, xb_w, xb_s)
 
-        wa_w = deal("wa_w", wa_w_raw, U16)
-        wa_s = deal("wa_s", wa_s_raw, U8)
+        wa_w = sb.tile([P, R], U16, name="wa_w", align_bytes=64)
+        wa_s = sb.tile([P, R], U8, name="wa_s", align_bytes=64)
+        deal(wa_w[:], wa_w_raw[:])
+        deal(wa_s[:], wa_s_raw[:])
         za = first_products("za", wa_w, E2M1, wa_s, xa_w, xa_s)
 
-        tf_picked = sb.tile([P, SLOTS, J], F32, name="tf_picked")
+        tf_picked = [sb.tile([P, SLOTS, HALF], F32, name="tf_picked%d" % h) for h in range(HALVES)]
         for t in range(SLOTS):
-            nc.scalar.activation(tf_picked[:, t, :], tf_sb[t][:].indirect(list_f[:]), ACT.Copy)
-        tv_picked = sb.tile([P, HALVES, I], F32, name="tv_picked")
-        for h in range(HALVES):
-            nc.scalar.activation(tv_picked[:, h, :], tv_sb[:, h, :].indirect(list_v[:]), ACT.Copy)
+            for h in range(HALVES):
+                entries = list_f[:, h * HALF // 16 : (h + 1) * HALF // 16]
+                nc.scalar.activation(tf_picked[h][:, t, :], tf_sb[t][:].indirect(entries), ACT.Copy)
 
         groups = HALF // BUNDLE
         sums, means, hb = [], [], []
@@ -154,18 +163,24 @@ def tile_list_meet_timestable_levelled_tabled_kernel(
             nc.vector.quantize_mx(out=hb_w[:, cols].bitcast(E4M3), scales=hb_s[:, cols], in_=hb[h][:])
         for h in range(HALVES):
             rows = slice(h * HALF, (h + 1) * HALF)
-            ha = sb.tile([P, HALF * SLOTS], BF16, name="ha%d" % h, align_bytes=64)
+            ha = sb.tile([P, HALF * SLOTS], BF16, name="ha%d" % h, tag="ha%d" % h, align_bytes=64)
             width = HALF if h < HALVES - 1 else HALF // 2
             for start in range(0, HALF, width):
                 nc.vector.tensor_tensor(
                     ha[:, start * SLOTS : (start + width) * SLOTS].rearrange("p (c e t) -> p c t e", e=4, t=SLOTS),
                     za[h][:, :, start : start + width].rearrange("p t (c e) -> p c t e", e=4),
-                    tf_picked[:, :, h * HALF + start : h * HALF + start + width].rearrange("p t (c e) -> p c t e", e=4),
+                    tf_picked[h][:, :, start : start + width].rearrange("p t (c e) -> p c t e", e=4),
                     ALU.mult,
                 )
             ha_w = sb.tile([P, HALF], U32, name="ha_w%d" % h, align_bytes=64)
             ha_s = sb.tile([P, HALF], U8, name="ha_s%d" % h, align_bytes=64)
             nc.vector.quantize_mx(out=ha_w[:].bitcast(E5M2), scales=ha_s[:], in_=ha[:])
+            if h < HALVES - 1:
+                tv_picked = sb.tile([P, I], F32, name="tv_picked%d" % h)
+                nc.scalar.activation(tv_picked[:], tv_sb[h][:].indirect(list_v[:]), ACT.Copy)
+            else:
+                tv_picked = sb.tile([P, I], F32, name="tv_picked%d" % h, tag="ha%d" % h, align_bytes=64)
+                nc.vector.tensor_copy(tv_picked[:], tv_sb[h][:].indirect(list_v[:]))
             result = sb.tile([P, I], F32, name="result%d" % h)
             width = I if h < HALVES - 1 else HALF
             for start in range(0, I, width):
@@ -181,7 +196,7 @@ def tile_list_meet_timestable_levelled_tabled_kernel(
                     stop=True,
                 )
                 name = "squashed%d_%d" % (h, start)
-                squashed = sb.tile([P, width], F32, name=name, tag="tv" if h == 0 else name)
+                squashed = sb.tile([P, width], F32, name=name, tag="tv0" if h == 0 else name)
                 nc.scalar.activation(squashed[:], score[:], ACT.Tanh, scale=0.04)
-                nc.vector.tensor_tensor(result[:, cols], squashed[:], tv_picked[:, h, cols], ALU.mult)
+                nc.vector.tensor_tensor(result[:, cols], squashed[:], tv_picked[:, cols], ALU.mult)
             nc.sync.dma_start(out[h * HALF : (h + 1) * HALF, :], result[:])

from contextlib import ExitStack

import concourse.mybir as mybir

F32 = mybir.dt.float32
BF16 = mybir.dt.bfloat16
I32 = mybir.dt.int32
U32 = mybir.dt.uint32
U16 = mybir.dt.uint16
U8 = mybir.dt.uint8
E2M1 = mybir.dt.float4_e2m1fn_x4
E5M2 = mybir.dt.float8_e5m2_x4
E4M3 = mybir.dt.float8_e4m3fn_x4
ALU = mybir.AluOpType
ACT = mybir.ActivationFunctionType

P = 128
K, T, J, I, R, C, Q = 512, 512, 256, 256, 512, 512, 512
SLOTS = 4
RUN = 8
BUNDLE = 8
HALF = 128
HALVES = 2

FLOPS = 2 * K * R * J + 2 * K * R * I + 2 * R * J * I


def tile_list_meet_timestable_levelled_tabled_kernel(
    tc, xt_words, xt_scales, wa_words, wa_scales, tf, wb_words, wb_scales, tv, offs, offs2, offs3, offs4, out
):
    nc = tc.nc
    with ExitStack() as ctx:
        sb = ctx.enter_context(tc.tile_pool(name="sb", bufs=1))
        ps = ctx.enter_context(tc.psum_pool(name="ps", bufs=1))

        def load_list(name, src):
            tile = sb.tile([P, 16], U16, name=name)
            nc.sync.dma_start(tile[:], src)
            return tile

        def load_scales(name, src):
            plane = sb.tile([P, R], U8, name=name, align_bytes=64)
            for q in range(4):
                nc.sync.dma_start(
                    plane[32 * q : 32 * q + 32, :].bitcast(I32),
                    src[:, 4 * q : 4 * q + 4, :].bitcast(I32).to_broadcast([8, 4, R // 4]),
                )
            return plane

        tf_rows = tf.rearrange("(b t m) c -> t b m c", t=SLOTS, m=RUN)
        tf_sb = []

        def load_factors(t):
            tile = sb.tile([P, C], F32, name="tf%d" % t)
            nc.sync.dma_start(tile[:], tf_rows[t])
            return tile

        wb_rows = wb_scales.bitcast(I32)
        wb_s_low = sb.tile([P, R], U8, name="wb_s_low", align_bytes=64)
        wb_s_high = sb.tile([P, R], U8, name="wb_s_high", align_bytes=64)
        nc.gpsimd.dma_start(wb_s_high[58:128, :].bitcast(I32), wb_rows[:, 2:16, :].to_broadcast([5, 14, R // 4]))
        list_b = load_list("list_b", offs3)
        xt_w = sb.tile([P, T], U16, name="xt_w", align_bytes=64)
        nc.sync.dma_start(xt_w[:].bitcast(I32), xt_words[0].bitcast(I32))
        xt_s = load_scales("xt_s", xt_scales)
        wb_w_raw = sb.tile([P, R], U32, name="wb_w_raw", align_bytes=64)
        nc.sync.dma_start(wb_w_raw[:].bitcast(I32), wb_words[0].rearrange("p c t -> p (c t)").bitcast(I32))
        nc.sync.dma_start(wb_s_low[0:70, :].bitcast(I32), wb_rows[:, 0:14, :].to_broadcast([5, 14, R // 4]))
        list_a = load_list("list_a", offs)
        list_f = load_list("list_f", offs2)
        tf_sb.append(load_factors(0))
        tf_sb.append(load_factors(1))
        wa_w_raw = sb.tile([P, R], U16, name="wa_w_raw", align_bytes=64)
        nc.sync.dma_start(wa_w_raw[:].bitcast(I32), wa_words[0].bitcast(I32))
        wa_s_raw = load_scales("wa_s_raw", wa_scales)
        tf_sb.append(load_factors(2))
        tf_sb.append(load_factors(3))
        list_v = load_list("list_v", offs4)
        tv_sb = []
        for h in range(HALVES):
            tile = sb.tile([P, Q], F32, name="tv%d" % h, tag="tv%d" % h)
            nc.sync.dma_start(tile[:], tv[h * HALF : (h + 1) * HALF, :])
            tv_sb.append(tile)

        def deal(dealt, raw):
            nc.scalar.copy(
                dealt.bitcast(U32).rearrange("p (t b w) -> p t b w", t=SLOTS, b=R // 32),
                raw.bitcast(U32).rearrange("p (b t w) -> p t b w", t=SLOTS, b=R // 32),
            )

        def pick(name, window, dtype, entries):
            picked = sb.tile([P, J], dtype, name=name, align_bytes=64)
            nc.vector.tensor_copy(picked[:], window[:].indirect(entries[:]))
            return picked

        def first_products(name, w_words, w_fmt, w_scales, x_words, x_scales):
            banks = []
            for h in range(HALVES):
                bank = ps.tile([P, SLOTS, HALF], F32, name="%s%d" % (name, h))
                cols = slice(h * HALF, (h + 1) * HALF)
                for t in range(SLOTS):
                    rows = slice(t * P, (t + 1) * P)
                    nc.tensor.matmul_mx(
                        out=bank[:, t, :],
                        lhsT=w_words[:, rows].bitcast(w_fmt),
                        lhsT_scale=w_scales[:, rows],
                        rhs=x_words[:, cols].bitcast(E2M1),
                        rhs_scale=x_scales[:, cols],
                        start=True,
                        stop=True,
                    )
                banks.append(bank)
            return banks

        xb_w = pick("xb_w", xt_w, U16, list_b)
        xb_s = pick("xb_s", xt_s, U8, list_b)
        xa_w = pick("xa_w", xt_w, U16, list_a)
        xa_s = pick("xa_s", xt_s, U8, list_a)
        wb_w = sb.tile([P, R], U32, name="wb_w", align_bytes=64)
        wb_s = sb.tile([P, R], U8, name="wb_s", align_bytes=64)
        deal(wb_w[:], wb_w_raw[:])
        deal(wb_s[0:64, :], wb_s_low[0:64, :])
        deal(wb_s[64:128, :], wb_s_high[64:128, :])
        zb = first_products("zb", wb_w, E5M2, wb_s, xb_w, xb_s)

        wa_w = sb.tile([P, R], U16, name="wa_w", align_bytes=64)
        wa_s = sb.tile([P, R], U8, name="wa_s", align_bytes=64)
        deal(wa_w[:], wa_w_raw[:])
        deal(wa_s[:], wa_s_raw[:])
        za = first_products("za", wa_w, E2M1, wa_s, xa_w, xa_s)

        tf_picked = [sb.tile([P, SLOTS, HALF], F32, name="tf_picked%d" % h) for h in range(HALVES)]
        for t in range(SLOTS):
            for h in range(HALVES):
                entries = list_f[:, h * HALF // 16 : (h + 1) * HALF // 16]
                nc.scalar.activation(tf_picked[h][:, t, :], tf_sb[t][:].indirect(entries), ACT.Copy)

        groups = HALF // BUNDLE
        sums, means, hb = [], [], []
        for h in range(HALVES):
            total = sb.tile([P, groups, SLOTS], F32, name="sums%d" % h)
            nc.vector.tensor_reduce(
                total[:], zb[h][:].rearrange("p t (g m) -> p g t m", m=BUNDLE), mybir.AxisListType.X, ALU.add
            )
            sums.append(total)
        for h in range(HALVES):
            mean = sb.tile([P, groups, SLOTS], F32, name="means%d" % h)
            nc.gpsimd.tensor_scalar(mean[:], sums[h][:], 1.0 / BUNDLE, 0.0, ALU.mult, ALU.add)
            means.append(mean)
        for h in range(HALVES):
            centred = sb.tile([P, HALF * SLOTS], BF16, name="hb%d" % h, align_bytes=64)
            nc.vector.tensor_tensor(
                centred[:].rearrange("p (g m t) -> p g m t", m=BUNDLE, t=SLOTS),
                zb[h][:].rearrange("p t (g m) -> p g m t", m=BUNDLE),
                means[h][:].unsqueeze(2).to_broadcast([P, groups, BUNDLE, SLOTS]),
                ALU.subtract,
            )
            hb.append(centred)
        hb_w = sb.tile([P, I], U32, name="hb_w", align_bytes=64)
        hb_s = sb.tile([P, I], U8, name="hb_s", align_bytes=64)
        for h in range(HALVES):
            cols = slice(h * HALF, (h + 1) * HALF)
            nc.vector.quantize_mx(out=hb_w[:, cols].bitcast(E4M3), scales=hb_s[:, cols], in_=hb[h][:])
        for h in range(HALVES):
            rows = slice(h * HALF, (h + 1) * HALF)
            ha = sb.tile([P, HALF * SLOTS], BF16, name="ha%d" % h, tag="ha%d" % h, align_bytes=64)
            width = HALF if h < HALVES - 1 else HALF // 2
            for start in range(0, HALF, width):
                nc.vector.tensor_tensor(
                    ha[:, start * SLOTS : (start + width) * SLOTS].rearrange("p (c e t) -> p c t e", e=4, t=SLOTS),
                    za[h][:, :, start : start + width].rearrange("p t (c e) -> p c t e", e=4),
                    tf_picked[h][:, :, start : start + width].rearrange("p t (c e) -> p c t e", e=4),
                    ALU.mult,
                )
            ha_w = sb.tile([P, HALF], U32, name="ha_w%d" % h, align_bytes=64)
            ha_s = sb.tile([P, HALF], U8, name="ha_s%d" % h, align_bytes=64)
            nc.vector.quantize_mx(out=ha_w[:].bitcast(E5M2), scales=ha_s[:], in_=ha[:])
            if h < HALVES - 1:
                tv_picked = sb.tile([P, I], F32, name="tv_picked%d" % h)
                nc.scalar.activation(tv_picked[:], tv_sb[h][:].indirect(list_v[:]), ACT.Copy)
            else:
                tv_picked = sb.tile([P, I], F32, name="tv_picked%d" % h, tag="ha%d" % h, align_bytes=64)
                nc.vector.tensor_copy(tv_picked[:], tv_sb[h][:].indirect(list_v[:]))
            result = sb.tile([P, I], F32, name="result%d" % h)
            width = I if h < HALVES - 1 else HALF
            for start in range(0, I, width):
                cols = slice(start, start + width)
                score = ps.tile([P, width], F32, name="score%d_%d" % (h, start))
                nc.tensor.matmul_mx(
                    out=score[:],
                    lhsT=ha_w[:].bitcast(E5M2),
                    lhsT_scale=ha_s[:],
                    rhs=hb_w[:, cols].bitcast(E4M3),
                    rhs_scale=hb_s[:, cols],
                    start=True,
                    stop=True,
                )
                name = "squashed%d_%d" % (h, start)
                squashed = sb.tile([P, width], F32, name=name, tag="tv0" if h == 0 else name)
                nc.scalar.activation(squashed[:], score[:], ACT.Tanh, scale=0.04)
                nc.vector.tensor_tensor(result[:, cols], squashed[:], tv_picked[:, cols], ALU.mult)
            nc.sync.dma_start(out[h * HALF : (h + 1) * HALF, :], result[:])
